import numpy as np
import ml_dtypes


def mxq(x, axis, fmt="e4m3"):
    dtype, down = {"e4m3": (ml_dtypes.float8_e4m3fn, 7), "e5m2": (ml_dtypes.float8_e5m2, 14)}[fmt]
    v = np.moveaxis(np.asarray(x, np.float32).astype(ml_dtypes.bfloat16).astype(np.float64), axis, -1)
    blocks = v.reshape(v.shape[:-1] + (-1, 32))
    amax = np.abs(blocks).max(-1, keepdims=True)
    byte = np.maximum(np.where(amax > 0, np.frexp(amax)[1] - 1 + 127, 0) - down, 1)
    scale = np.exp2(byte - 127.0)
    codes = (blocks / scale).astype(np.float32).astype(dtype).astype(np.float64)
    return np.moveaxis((codes * scale).reshape(v.shape), -1, axis)


WIDE = False


def mx_kscale(k):
    if not WIDE:
        return np.ones(k)
    levels = np.array([10, -10, 5, -5, 0])
    if k % 512:
        return np.exp2(np.random.permutation(np.resize(levels, k // 32))).repeat(32)
    a = np.empty((k // 512, 16))
    for p in range(k // 512):
        a[p, :8] = np.random.permutation(np.resize(levels, 8))
        for g in range(8):
            far = levels[np.abs(levels - a[p, g]) >= 10]
            a[p, g + 8] = far[np.random.randint(len(far))]
    return np.exp2(a.ravel()).repeat(32)


def f64(x):
    return np.asarray(x).astype(np.float64)


def striped(idx):
    return np.tile(np.asarray(idx).reshape(-1, 16).T, (8, 1)).astype(np.uint16)


def unstriped(offs):
    return offs[:16].T.reshape(-1).astype(np.int64)


E2M1 = np.array([0.0, 0.5, 1.0, 1.5, 2.0, 3.0, 4.0, 6.0, -0.0, -0.5, -1.0, -1.5, -2.0, -3.0, -4.0, -6.0])


def pack_weight(w, fmt):
    k, n = w.shape
    w = f64(np.asarray(w, np.float32).astype(ml_dtypes.bfloat16)).reshape(k // 32, 32, n)
    amax = np.abs(w).max(1)
    if fmt == "e4m3":
        byte = np.frexp(amax)[1] - 1 + 127 - 7
    else:
        mant, ex = np.frexp(amax / 6.0)
        byte = np.where(mant > 0.5, ex, ex - 1) + 127
    byte = np.clip(np.where(amax > 0, byte, 1), 1, 254)
    scaled = (w * np.exp2(127.0 - byte)[:, None, :]).reshape(k, n).astype(np.float32)
    by_word = np.ascontiguousarray(scaled.reshape(k // 512, 128, 4, n).transpose(0, 1, 3, 2))
    if fmt == "e4m3":
        words = by_word.astype(ml_dtypes.float8_e4m3fn).view(np.uint8)
    else:
        c = by_word.astype(ml_dtypes.float4_e2m1fn).view(np.uint8) & 0xF
        words = (c[..., 0::2] | (c[..., 1::2] << 4)).reshape(k // 512, 128, 2 * n)
    return np.ascontiguousarray(words), np.ascontiguousarray(byte.astype(np.uint8).reshape(k // 512, 16, n))


def unpack_weight(words, scales, fmt):
    g, _, n = scales.shape
    words = np.ascontiguousarray(words).reshape(g, 128, n, -1)
    if fmt == "e4m3":
        vals = words.view(ml_dtypes.float8_e4m3fn).astype(np.float64)
    else:
        nib = np.empty((g, 128, n, 4), np.uint8)
        nib[..., 0::2] = words & 0xF
        nib[..., 1::2] = words >> 4
        vals = E2M1[nib]
    vals = vals * np.repeat(np.exp2(scales.astype(np.float64) - 127.0), 8, axis=1)[..., None]
    return vals.transpose(0, 1, 3, 2).reshape(g * 512, n)


D, T, I, Q, E, Z, M, C = 512, 2048, 512, 256, 512, 1024, 1024, 512


def setup_inputs():
    n = np.random.standard_normal
    idx = np.random.permutation(T)[:I]
    idx2 = np.random.permutation(Z)[:I]
    idx3 = np.random.permutation(M)[:Q]
    fd = mx_kscale(D)
    fi = mx_kscale(I)
    fc = mx_kscale(C)
    ti = np.ones(T)
    ti[idx] = fi
    keysp = pack_weight(n((D, T)) / fd[:, None], "e4m3")
    return {
        "query": (n((D, Q)) * 1.0 / np.sqrt(D) * fd[:, None]).astype(np.float32),
        "keys_words": keysp[0],
        "keys_scales": keysp[1],
        "earl": (np.random.uniform(0.3, 1.7, (Q, Z))).astype(np.float32),
        "os": (np.random.uniform(0.02, 0.08, (1, I)) * fi).astype(np.float32),
        "vals": (n((E, T)) / ti).astype(np.float32),
        "wm": (n((C, E)) * 1.0 / np.sqrt(C) * fc[:, None]).astype(np.float32),
        "mstore": (n((C, M)) / fc[:, None]).astype(np.float32),
        "offs": striped(idx),
        "offs2": striped(idx2),
        "offs3": striped(idx3),
    }


def reference(query, keys_words, keys_scales, earl, os, vals, wm, mstore, offs, offs2, offs3):
    idx = unstriped(offs)
    idx2 = unstriped(offs2)
    idx3 = unstriped(offs3)
    keysu = unpack_weight(keys_words, keys_scales, "e4m3")
    queryq = mxq(f64(query), 0, "e4m3")
    keysidxg = keysu[:, idx]
    a = queryq.T @ keysidxg
    w = a * f64(earl)[:, idx2]
    wo1 = w * f64(os)
    wt1 = wo1.T
    vt1 = f64(vals)[:, idx].T
    vt1q = mxq(vt1, 0, "e4m3")
    wt1q = mxq(wt1, 0, "e4m3")
    o = vt1q.T @ wt1q
    wmq = mxq(f64(wm), 0, "e4m3")
    mstoreq = mxq(f64(mstore), 0, "e4m3")
    me = wmq.T @ mstoreq
    y = o * me[:, idx3]
    return y

@@ -1,0 +1,174 @@
+from contextlib import ExitStack
+
+import concourse.mybir as mybir
+from concourse.masks import make_identity
+
+D, T, I, Q, E, Z, M, C = 512, 2048, 512, 256, 512, 1024, 1024, 512
+FLOPS = 2 * (D * Q * I + I * E * Q + C * E * M)
+
+F32 = mybir.dt.float32
+BF16 = mybir.dt.bfloat16
+I32 = mybir.dt.int32
+U32 = mybir.dt.uint32
+U16 = mybir.dt.uint16
+U8 = mybir.dt.uint8
+FP8X4 = mybir.dt.float8_e4m3fn_x4
+MULT = mybir.AluOpType.mult
+COPY = mybir.ActivationFunctionType.Copy
+
+P = 128
+PACK = 4
+BANK = 512
+
+
+def tile_attend_earliertable_remembered_lean_kernel(
+    tc, query, keys_words, keys_scales, earl, slot_factor, vals, wm, mstore, offs, offs2, offs3, out
+):
+    nc = tc.nc
+    e_blocks = E // P
+    q_blocks = Q // P
+    m_halves = M // BANK
+
+    with ExitStack() as ctx:
+        lists = ctx.enter_context(tc.tile_pool(name="lists", bufs=1))
+        sb = ctx.enter_context(tc.tile_pool(name="sb", bufs=1))
+        psum = ctx.enter_context(tc.psum_pool(name="psum", bufs=2))
+
+        def load_rows(name, rows):
+            width = rows.shape[1]
+            raw = sb.tile([P, PACK, width], F32, name=name)
+            nc.sync.dma_start(out=raw[:], in_=rows.rearrange("(p j) w -> p j w", j=PACK))
+            return raw
+
+        def interleave(name, raw):
+            width = raw.shape[2]
+            grouped = sb.tile([P, width, PACK], BF16, name=name, align_bytes=64)
+            nc.vector.tensor_copy(
+                out=grouped[:].rearrange("p (c i) t -> p c t i", i=4),
+                in_=raw[:].rearrange("p t (c i) -> p c t i", i=4),
+            )
+            return grouped
+
+        def quantize(name, grouped):
+            width = grouped.shape[1]
+            codes = sb.tile([P, width], U32, name=name + "_codes", align_bytes=64)
+            scales = sb.tile([P, width], U8, name=name + "_scales", align_bytes=64)
+            nc.vector.quantize_mx(
+                out=codes[:].bitcast(FP8X4), scales=scales[:], in_=grouped[:].rearrange("p w t -> p (w t)")
+            )
+            return codes, scales
+
+        def product(acc, stationary, cols, moving):
+            nc.tensor.matmul_mx(
+                out=acc,
+                lhsT=stationary[0][:, cols].bitcast(FP8X4),
+                lhsT_scale=stationary[1][:, cols],
+                rhs=moving[0][:].bitcast(FP8X4),
+                rhs_scale=moving[1][:],
+                start=True,
+                stop=True,
+            )
+
+        key_bytes = sb.tile([P, T], U8, name="key_bytes", align_bytes=64)
+        nc.gpsimd.memset(key_bytes[:].bitcast(U32), 0)
+        ident = sb.tile([P, P], F32, name="ident")
+        make_identity(nc, ident[:])
+
+        wm_raw = load_rows("wm_raw", wm)
+        ms_raw = [load_rows("ms_raw0", mstore[:, 0:BANK])]
+        list3 = lists.tile([P, Q // 16], U16, name="list3")
+        nc.sync.dma_start(list3[:], offs3)
+        list1 = lists.tile([P, I // 16], U16, name="list1")
+        nc.sync.dma_start(list1[:], offs)
+        list2 = lists.tile([P, I // 16], U16, name="list2")
+        nc.sync.dma_start(list2[:], offs2)
+        ms_raw.append(load_rows("ms_raw1", mstore[:, BANK:M]))
+        factor = sb.tile([P, PACK], F32, name="factor")
+        nc.sync.dma_start(out=factor[:], in_=slot_factor.rearrange("o (p t) -> p (o t)", t=PACK))
+        for quad in range(4):
+            nc.scalar.dma_start(
+                out=key_bytes[32 * quad : 32 * quad + 4, :].bitcast(I32),
+                in_=keys_scales[0, 4 * quad : 4 * quad + 4, :].bitcast(I32),
+            )
+        q_raw = load_rows("q_raw", query)
+        key_words = sb.tile([P, T], U32, name="key_words", align_bytes=64)
+        nc.sync.dma_start(
+            out=key_words[:].bitcast(I32), in_=keys_words[0].rearrange("p n t -> p (n t)").bitcast(I32)
+        )
+        earl_sb = []
+        for qb in range(q_blocks):
+            table = sb.tile([P, Z], F32, name="earl%d" % qb)
+            nc.sync.dma_start(out=table[:], in_=earl[qb * P : (qb + 1) * P, :])
+            earl_sb.append(table)
+        vals_sb = []
+        for eb in range(e_blocks):
+            pool_rows = sb.tile([P, T], F32, name="vals%d" % eb)
+            nc.sync.dma_start(out=pool_rows[:], in_=vals[eb * P : (eb + 1) * P, :])
+            vals_sb.append(pool_rows)
+
+        wm_q = quantize("wm", interleave("wm_bf", wm_raw))
+        me_sb = [sb.tile([P, M], F32, name="me%d" % eb) for eb in range(e_blocks)]
+        for h in range(m_halves):
+            ms_q = quantize("ms%d" % h, interleave("ms_bf%d" % h, ms_raw[h]))
+            for eb in range(e_blocks):
+                me_ps = psum.tile([P, BANK], F32, name="me_ps")
+                product(me_ps[:], wm_q, slice(eb * P, (eb + 1) * P), ms_q)
+                nc.scalar.copy(out=me_sb[eb][:, h * BANK : (h + 1) * BANK], in_=me_ps[:])
+
+        q_q = quantize("q", interleave("q_bf", q_raw))
+        picked_words = sb.tile([P, I], U32, name="picked_words", align_bytes=64)
+        nc.vector.tensor_copy(picked_words[:], key_words[:].indirect(list1[:]))
+        picked_bytes = sb.tile([P, I], U8, name="picked_bytes", align_bytes=64)
+        nc.vector.tensor_copy(picked_bytes[:], key_bytes[:].indirect(list1[:]))
+        scores = []
+        for qb in range(q_blocks):
+            a_ps = psum.tile([P, I], F32, name="a_ps", tag="score")
+            product(a_ps[:], q_q, slice(qb * P, (qb + 1) * P), (picked_words, picked_bytes))
+            scores.append(a_ps)
+
+        me_picked = []
+        for eb in range(e_blocks):
+            picked = sb.tile([P, Q], F32, name="me_picked%d" % eb)
+            nc.vector.tensor_copy(picked[:], me_sb[eb][:].indirect(list3[:]))
+            me_picked.append(picked)
+
+        w_bf = sb.tile([P, Q, PACK], BF16, name="w_bf", align_bytes=64)
+        w_rows = []
+        for qb in range(q_blocks):
+            earl_picked = sb.tile([P, I], F32, name="earl_picked%d" % qb)
+            nc.scalar.activation(earl_picked[:], earl_sb[qb][:].indirect(list2[:]), COPY)
+            w_row = sb.tile([P, I], F32, name="w_row%d" % qb)
+            nc.vector.tensor_tensor(w_row[:], scores[qb][:], earl_picked[:], MULT)
+            w_rows.append(w_row)
+        for qb in range(q_blocks):
+            wt_ps = psum.tile([P, PACK, P], F32, name="wt_ps", tag="score")
+            for t in range(PACK):
+                nc.tensor.transpose(wt_ps[:, t, :], w_rows[qb][:, t:I:PACK], ident[:])
+            nc.vector.tensor_tensor(
+                w_bf[:, qb * P : (qb + 1) * P, :],
+                wt_ps[:].rearrange("p t q -> p q t"),
+                factor[:].unsqueeze(1).to_broadcast([P, P, PACK]),
+                MULT,
+            )
+        w_q = quantize("w", w_bf)
+
+        for eb in range(e_blocks):
+            v_picked = sb.tile([P, I], BF16, name="v_picked%d" % eb)
+            if eb < e_blocks - 1:
+                nc.scalar.activation(v_picked[:], vals_sb[eb][:].indirect(list1[:]), COPY)
+            else:
+                half = I // 2
+                nc.scalar.activation(v_picked[:, :half], vals_sb[eb][:].indirect(list1[:, : half // 16]), COPY)
+                nc.vector.tensor_copy(v_picked[:, half:], vals_sb[eb][:].indirect(list1[:, half // 16 :]))
+            pairs = v_picked[:].bitcast(F32)
+            vt_ps = psum.tile([P, 2, P], F32, name="vt_ps")
+            for u in range(2):
+                nc.tensor.transpose(vt_ps[:, u, :], pairs[:, u : I // 2 : 2], ident[:])
+            v_bf = sb.tile([P, P, PACK], BF16, name="v_bf%d" % eb, align_bytes=64)
+            nc.scalar.copy(out=v_bf[:].bitcast(F32), in_=vt_ps[:].rearrange("p u e -> p e u"))
+            v_q = quantize("v%d" % eb, v_bf)
+            o_ps = psum.tile([P, Q], F32, name="o_ps")
+            product(o_ps[:], v_q, slice(0, P), w_q)
+            result = sb.tile([P, Q], F32, name="result%d" % eb)
+            nc.vector.tensor_tensor(result[:], o_ps[:], me_picked[eb][:], MULT)
+            nc.sync.dma_start(out=out[eb * P : (eb + 1) * P, :], in_=result[:])

@@ -32,7 +32,7 @@ def tile_attend_earliertable_remembered_lean_kernel(
     with ExitStack() as ctx:
         lists = ctx.enter_context(tc.tile_pool(name="lists", bufs=1))
         sb = ctx.enter_context(tc.tile_pool(name="sb", bufs=1))
-        psum = ctx.enter_context(tc.psum_pool(name="psum", bufs=2))
+        psum = ctx.enter_context(tc.psum_pool(name="psum", bufs=1))
 
         def load_rows(name, rows):
             width = rows.shape[1]
@@ -40,13 +40,19 @@ def tile_attend_earliertable_remembered_lean_kernel(
             nc.sync.dma_start(out=raw[:], in_=rows.rearrange("(p j) w -> p j w", j=PACK))
             return raw
 
-        def interleave(name, raw):
+        def interleave(name, raw, on_scalar=0):
             width = raw.shape[2]
             grouped = sb.tile([P, width, PACK], BF16, name=name, align_bytes=64)
+            cut = width - on_scalar
             nc.vector.tensor_copy(
-                out=grouped[:].rearrange("p (c i) t -> p c t i", i=4),
-                in_=raw[:].rearrange("p t (c i) -> p c t i", i=4),
+                out=grouped[:, :cut, :].rearrange("p (c i) t -> p c t i", i=4),
+                in_=raw[:, :, :cut].rearrange("p t (c i) -> p c t i", i=4),
             )
+            if on_scalar:
+                nc.scalar.copy(
+                    out=grouped[:, cut:, :].rearrange("p (c i) t -> p c t i", i=4),
+                    in_=raw[:, :, cut:].rearrange("p t (c i) -> p c t i", i=4),
+                )
             return grouped
 
         def quantize(name, grouped):
@@ -58,13 +64,13 @@ def tile_attend_earliertable_remembered_lean_kernel(
             )
             return codes, scales
 
-        def product(acc, stationary, cols, moving):
+        def product(acc, stationary, cols, moving, moving_cols=slice(None)):
             nc.tensor.matmul_mx(
                 out=acc,
                 lhsT=stationary[0][:, cols].bitcast(FP8X4),
                 lhsT_scale=stationary[1][:, cols],
-                rhs=moving[0][:].bitcast(FP8X4),
-                rhs_scale=moving[1][:],
+                rhs=moving[0][:, moving_cols].bitcast(FP8X4),
+                rhs_scale=moving[1][:, moving_cols],
                 start=True,
                 stop=True,
             )
@@ -74,63 +80,67 @@ def tile_attend_earliertable_remembered_lean_kernel(
         ident = sb.tile([P, P], F32, name="ident")
         make_identity(nc, ident[:])
 
-        wm_raw = load_rows("wm_raw", wm)
-        ms_raw = [load_rows("ms_raw0", mstore[:, 0:BANK])]
-        list3 = lists.tile([P, Q // 16], U16, name="list3")
-        nc.sync.dma_start(list3[:], offs3)
-        list1 = lists.tile([P, I // 16], U16, name="list1")
-        nc.sync.dma_start(list1[:], offs)
-        list2 = lists.tile([P, I // 16], U16, name="list2")
-        nc.sync.dma_start(list2[:], offs2)
-        ms_raw.append(load_rows("ms_raw1", mstore[:, BANK:M]))
-        factor = sb.tile([P, PACK], F32, name="factor")
-        nc.sync.dma_start(out=factor[:], in_=slot_factor.rearrange("o (p t) -> p (o t)", t=PACK))
-        for quad in range(4):
+        def load_list(name, source):
+            offsets = lists.tile(list(source.shape), U16, name=name)
+            nc.sync.dma_start(offsets[:], source)
+            return offsets
+
+        def load_block(name, rows):
+            block = sb.tile([P, rows.shape[1]], F32, name=name, align_bytes=64)
+            nc.sync.dma_start(out=block[:], in_=rows)
+            return block
+
+        list1 = load_list("list1", offs)
+        byte_rows = sb.tile([P, 2, T // 4], I32, name="byte_rows")
+        for pair in range(2):
             nc.scalar.dma_start(
-                out=key_bytes[32 * quad : 32 * quad + 4, :].bitcast(I32),
-                in_=keys_scales[0, 4 * quad : 4 * quad + 4, :].bitcast(I32),
+                out=byte_rows[64 * pair : 64 * pair + 4, :, :],
+                in_=keys_scales[0, 8 * pair : 8 * pair + 8, :].bitcast(I32).rearrange("(a r) n -> r a n", a=2),
             )
-        q_raw = load_rows("q_raw", query)
+        factor = sb.tile([P, PACK], F32, name="factor")
+        nc.scalar.dma_start(out=factor[:], in_=slot_factor.rearrange("o (p t) -> p (o t)", t=PACK))
+        wm_raw = load_rows("wm_raw", wm)
+        ms_raw = [load_rows("ms_raw%d" % h, mstore[:, h * BANK : (h + 1) * BANK]) for h in range(m_halves)]
         key_words = sb.tile([P, T], U32, name="key_words", align_bytes=64)
         nc.sync.dma_start(
             out=key_words[:].bitcast(I32), in_=keys_words[0].rearrange("p n t -> p (n t)").bitcast(I32)
         )
-        earl_sb = []
-        for qb in range(q_blocks):
-            table = sb.tile([P, Z], F32, name="earl%d" % qb)
-            nc.sync.dma_start(out=table[:], in_=earl[qb * P : (qb + 1) * P, :])
-            earl_sb.append(table)
-        vals_sb = []
-        for eb in range(e_blocks):
-            pool_rows = sb.tile([P, T], F32, name="vals%d" % eb)
-            nc.sync.dma_start(out=pool_rows[:], in_=vals[eb * P : (eb + 1) * P, :])
-            vals_sb.append(pool_rows)
+        list3 = load_list("list3", offs3)
+        q_raw = load_rows("q_raw", query)
+        list2 = load_list("list2", offs2)
+        earl_sb = [load_block("earl%d" % qb, earl[qb * P : (qb + 1) * P, :]) for qb in range(q_blocks)]
+        vals_sb = [load_block("vals%d" % eb, vals[eb * P : (eb + 1) * P, :]) for eb in range(e_blocks)]
 
-        wm_q = quantize("wm", interleave("wm_bf", wm_raw))
-        me_sb = [sb.tile([P, M], F32, name="me%d" % eb) for eb in range(e_blocks)]
-        for h in range(m_halves):
-            ms_q = quantize("ms%d" % h, interleave("ms_bf%d" % h, ms_raw[h]))
-            for eb in range(e_blocks):
-                me_ps = psum.tile([P, BANK], F32, name="me_ps")
-                product(me_ps[:], wm_q, slice(eb * P, (eb + 1) * P), ms_q)
-                nc.scalar.copy(out=me_sb[eb][:, h * BANK : (h + 1) * BANK], in_=me_ps[:])
-
-        q_q = quantize("q", interleave("q_bf", q_raw))
-        picked_words = sb.tile([P, I], U32, name="picked_words", align_bytes=64)
-        nc.vector.tensor_copy(picked_words[:], key_words[:].indirect(list1[:]))
+        for quad in range(4):
+            first = 64 * (quad // 2)
+            nc.vector.tensor_copy(
+                key_bytes[32 * quad : 32 * quad + 4, :].bitcast(I32), byte_rows[first : first + 4, quad % 2, :]
+            )
         picked_bytes = sb.tile([P, I], U8, name="picked_bytes", align_bytes=64)
         nc.vector.tensor_copy(picked_bytes[:], key_bytes[:].indirect(list1[:]))
+
+        wm_q = quantize("wm", interleave("wm_bf", wm_raw, 256))
+        me_sb = [sb.tile([P, M], F32, name="me%d" % eb) for eb in range(e_blocks)]
+        def memories(h, ms_q):
+            for eb in range(e_blocks):
+                me_ps = psum.tile([P, BANK], F32, name="me_ps", tag="block%d" % eb)
+                product(me_ps[:], wm_q, slice(eb * P, (eb + 1) * P), ms_q)
+                if h == 1 and eb >= 2:
+                    nc.vector.tensor_copy(out=me_sb[eb][:, h * BANK : (h + 1) * BANK], in_=me_ps[:])
+                else:
+                    nc.scalar.copy(out=me_sb[eb][:, h * BANK : (h + 1) * BANK], in_=me_ps[:])
+
+        memories(0, quantize("ms0", interleave("ms_bf0", ms_raw[0], 176)))
+        ms1_q = quantize("ms1", interleave("ms_bf1", ms_raw[1]))
+
+        picked_words = sb.tile([P, I], U32, name="picked_words", align_bytes=64)
+        nc.vector.tensor_copy(picked_words[:], key_words[:].indirect(list1[:]))
+        q_q = quantize("q", interleave("q_bf", q_raw))
         scores = []
         for qb in range(q_blocks):
-            a_ps = psum.tile([P, I], F32, name="a_ps", tag="score")
+            a_ps = psum.tile([P, I], F32, name="a_ps", tag="score%d" % qb)
             product(a_ps[:], q_q, slice(qb * P, (qb + 1) * P), (picked_words, picked_bytes))
             scores.append(a_ps)
-
-        me_picked = []
-        for eb in range(e_blocks):
-            picked = sb.tile([P, Q], F32, name="me_picked%d" % eb)
-            nc.vector.tensor_copy(picked[:], me_sb[eb][:].indirect(list3[:]))
-            me_picked.append(picked)
 
         w_bf = sb.tile([P, Q, PACK], BF16, name="w_bf", align_bytes=64)
         w_rows = []
@@ -138,12 +148,17 @@ def tile_attend_earliertable_remembered_lean_kernel(
             earl_picked = sb.tile([P, I], F32, name="earl_picked%d" % qb)
             nc.scalar.activation(earl_picked[:], earl_sb[qb][:].indirect(list2[:]), COPY)
             w_row = sb.tile([P, I], F32, name="w_row%d" % qb)
-            nc.vector.tensor_tensor(w_row[:], scores[qb][:], earl_picked[:], MULT)
+            nc.vector.tensor_tensor(
+                w_row[:].rearrange("p (t c i) -> p c t i", t=PACK, i=4),
+                scores[qb][:].rearrange("p (c i t) -> p c t i", t=PACK, i=4),
+                earl_picked[:].rearrange("p (c i t) -> p c t i", t=PACK, i=4),
+                MULT,
+            )
             w_rows.append(w_row)
         for qb in range(q_blocks):
-            wt_ps = psum.tile([P, PACK, P], F32, name="wt_ps", tag="score")
+            wt_ps = psum.tile([P, PACK, P], F32, name="wt_ps", tag="score%d" % qb)
             for t in range(PACK):
-                nc.tensor.transpose(wt_ps[:, t, :], w_rows[qb][:, t:I:PACK], ident[:])
+                nc.tensor.transpose(wt_ps[:, t, :], w_rows[qb][:, t * P : (t + 1) * P], ident[:])
             nc.vector.tensor_tensor(
                 w_bf[:, qb * P : (qb + 1) * P, :],
                 wt_ps[:].rearrange("p t q -> p q t"),
@@ -152,23 +167,48 @@ def tile_attend_earliertable_remembered_lean_kernel(
             )
         w_q = quantize("w", w_bf)
 
+        memories(1, ms1_q)
+        picked_by_scalar = sb.tile([P, 2, Q], F32, name="picked_by_scalar", tag="earl1", align_bytes=64)
+        picked_by_vector = sb.tile([P, 2, Q], F32, name="picked_by_vector", tag="w_bf", align_bytes=64)
+        me_picked = []
         for eb in range(e_blocks):
+            if eb < 2:
+                picked = picked_by_scalar[:, eb, :]
+                nc.scalar.activation(picked, me_sb[eb][:].indirect(list3[:]), COPY)
+            else:
+                picked = picked_by_vector[:, eb - 2, :]
+                nc.vector.tensor_copy(picked, me_sb[eb][:].indirect(list3[:]))
+            me_picked.append(picked)
+
+        def turn_values(eb):
             v_picked = sb.tile([P, I], BF16, name="v_picked%d" % eb)
-            if eb < e_blocks - 1:
+            if eb < e_blocks - 2:
                 nc.scalar.activation(v_picked[:], vals_sb[eb][:].indirect(list1[:]), COPY)
             else:
                 half = I // 2
                 nc.scalar.activation(v_picked[:, :half], vals_sb[eb][:].indirect(list1[:, : half // 16]), COPY)
                 nc.vector.tensor_copy(v_picked[:, half:], vals_sb[eb][:].indirect(list1[:, half // 16 :]))
             pairs = v_picked[:].bitcast(F32)
-            vt_ps = psum.tile([P, 2, P], F32, name="vt_ps")
+            vt_ps = psum.tile([P, 2, P], F32, name="vt_ps", tag="block%d" % eb)
             for u in range(2):
                 nc.tensor.transpose(vt_ps[:, u, :], pairs[:, u : I // 2 : 2], ident[:])
-            v_bf = sb.tile([P, P, PACK], BF16, name="v_bf%d" % eb, align_bytes=64)
+            v_bf = sb.tile([P, P, PACK], BF16, name="v_bf", tag="vals%d" % ((eb + 1) % e_blocks), align_bytes=64)
             nc.scalar.copy(out=v_bf[:].bitcast(F32), in_=vt_ps[:].rearrange("p u e -> p e u"))
-            v_q = quantize("v%d" % eb, v_bf)
-            o_ps = psum.tile([P, Q], F32, name="o_ps")
-            product(o_ps[:], v_q, slice(0, P), w_q)
-            result = sb.tile([P, Q], F32, name="result%d" % eb)
-            nc.vector.tensor_tensor(result[:], o_ps[:], me_picked[eb][:], MULT)
-            nc.sync.dma_start(out=out[eb * P : (eb + 1) * P, :], in_=result[:])
+            return quantize("v%d" % eb, v_bf)
+
+        def finish(eb, v_q):
+            result = sb.tile([P, Q], F32, name="result", tag="vals%d" % ((eb + 2) % e_blocks), align_bytes=64)
+            pieces = 2 if eb == e_blocks - 1 else 1
+            width = Q // pieces
+            for piece in range(pieces):
+                cols = slice(piece * width, (piece + 1) * width)
+                o_ps = psum.tile([P, width], F32, name="o_ps", tag="block%d" % ((eb + 1 + piece) % e_blocks) if pieces > 1 else "score%d" % (eb % 2))
+                product(o_ps[:], v_q, slice(0, P), w_q, cols)
+                nc.vector.tensor_tensor(result[:, cols], o_ps[:], me_picked[eb][:, cols], MULT)
+                nc.sync.dma_start(out=out[eb * P : (eb + 1) * P, cols], in_=result[:, cols])
+
+        v_q = [turn_values(0)]
+        for eb in range(1, e_blocks):
+            v_q.append(turn_values(eb))
+        for eb in range(e_blocks):
+            finish(eb, v_q[eb])

@@ -64,13 +64,13 @@ def tile_attend_earliertable_remembered_lean_kernel(
             )
             return codes, scales
 
-        def product(acc, stationary, cols, moving, moving_cols=slice(None)):
+        def product(acc, stationary, cols, moving):
             nc.tensor.matmul_mx(
                 out=acc,
                 lhsT=stationary[0][:, cols].bitcast(FP8X4),
                 lhsT_scale=stationary[1][:, cols],
-                rhs=moving[0][:, moving_cols].bitcast(FP8X4),
-                rhs_scale=moving[1][:, moving_cols],
+                rhs=moving[0][:].bitcast(FP8X4),
+                rhs_scale=moving[1][:],
                 start=True,
                 stop=True,
             )
@@ -197,15 +197,11 @@ def tile_attend_earliertable_remembered_lean_kernel(
             return quantize("v%d" % eb, v_bf)
 
         def finish(eb, v_q):
+            o_ps = psum.tile([P, Q], F32, name="o_ps", tag="score%d" % (eb % 2))
+            product(o_ps[:], v_q, slice(0, P), w_q)
             result = sb.tile([P, Q], F32, name="result", tag="vals%d" % ((eb + 2) % e_blocks), align_bytes=64)
-            pieces = 2 if eb == e_blocks - 1 else 1
-            width = Q // pieces
-            for piece in range(pieces):
-                cols = slice(piece * width, (piece + 1) * width)
-                o_ps = psum.tile([P, width], F32, name="o_ps", tag="block%d" % ((eb + 1 + piece) % e_blocks) if pieces > 1 else "score%d" % (eb % 2))
-                product(o_ps[:], v_q, slice(0, P), w_q, cols)
-                nc.vector.tensor_tensor(result[:, cols], o_ps[:], me_picked[eb][:, cols], MULT)
-                nc.sync.dma_start(out=out[eb * P : (eb + 1) * P, cols], in_=result[:, cols])
+            nc.vector.tensor_tensor(result[:], o_ps[:], me_picked[eb], MULT)
+            nc.sync.dma_start(out=out[eb * P : (eb + 1) * P, :], in_=result[:])
 
         v_q = [turn_values(0)]
         for eb in range(1, e_blocks):

from contextlib import ExitStack

import concourse.mybir as mybir
from concourse.masks import make_identity

D, T, I, Q, E, Z, M, C = 512, 2048, 512, 256, 512, 1024, 1024, 512
FLOPS = 2 * (D * Q * I + I * E * Q + C * E * M)

F32 = mybir.dt.float32
BF16 = mybir.dt.bfloat16
I32 = mybir.dt.int32
U32 = mybir.dt.uint32
U16 = mybir.dt.uint16
U8 = mybir.dt.uint8
FP8X4 = mybir.dt.float8_e4m3fn_x4
MULT = mybir.AluOpType.mult
COPY = mybir.ActivationFunctionType.Copy

P = 128
PACK = 4
BANK = 512


def tile_attend_earliertable_remembered_lean_kernel(
    tc, query, keys_words, keys_scales, earl, slot_factor, vals, wm, mstore, offs, offs2, offs3, out
):
    nc = tc.nc
    e_blocks = E // P
    q_blocks = Q // P
    m_halves = M // BANK

    with ExitStack() as ctx:
        lists = ctx.enter_context(tc.tile_pool(name="lists", bufs=1))
        sb = ctx.enter_context(tc.tile_pool(name="sb", bufs=1))
        psum = ctx.enter_context(tc.psum_pool(name="psum", bufs=1))

        def load_rows(name, rows):
            width = rows.shape[1]
            raw = sb.tile([P, PACK, width], F32, name=name)
            nc.sync.dma_start(out=raw[:], in_=rows.rearrange("(p j) w -> p j w", j=PACK))
            return raw

        def interleave(name, raw, on_scalar=0):
            width = raw.shape[2]
            grouped = sb.tile([P, width, PACK], BF16, name=name, align_bytes=64)
            cut = width - on_scalar
            nc.vector.tensor_copy(
                out=grouped[:, :cut, :].rearrange("p (c i) t -> p c t i", i=4),
                in_=raw[:, :, :cut].rearrange("p t (c i) -> p c t i", i=4),
            )
            if on_scalar:
                nc.scalar.copy(
                    out=grouped[:, cut:, :].rearrange("p (c i) t -> p c t i", i=4),
                    in_=raw[:, :, cut:].rearrange("p t (c i) -> p c t i", i=4),
                )
            return grouped

        def quantize(name, grouped):
            width = grouped.shape[1]
            codes = sb.tile([P, width], U32, name=name + "_codes", align_bytes=64)
            scales = sb.tile([P, width], U8, name=name + "_scales", align_bytes=64)
            nc.vector.quantize_mx(
                out=codes[:].bitcast(FP8X4), scales=scales[:], in_=grouped[:].rearrange("p w t -> p (w t)")
            )
            return codes, scales

        def product(acc, stationary, cols, moving):
            nc.tensor.matmul_mx(
                out=acc,
                lhsT=stationary[0][:, cols].bitcast(FP8X4),
                lhsT_scale=stationary[1][:, cols],
                rhs=moving[0][:].bitcast(FP8X4),
                rhs_scale=moving[1][:],
                start=True,
                stop=True,
            )

        key_bytes = sb.tile([P, T], U8, name="key_bytes", align_bytes=64)
        nc.gpsimd.memset(key_bytes[:].bitcast(U32), 0)
        ident = sb.tile([P, P], F32, name="ident")
        make_identity(nc, ident[:])

        def load_list(name, source):
            offsets = lists.tile(list(source.shape), U16, name=name)
            nc.sync.dma_start(offsets[:], source)
            return offsets

        def load_block(name, rows):
            block = sb.tile([P, rows.shape[1]], F32, name=name, align_bytes=64)
            nc.sync.dma_start(out=block[:], in_=rows)
            return block

        list1 = load_list("list1", offs)
        byte_rows = sb.tile([P, 2, T // 4], I32, name="byte_rows")
        for pair in range(2):
            nc.scalar.dma_start(
                out=byte_rows[64 * pair : 64 * pair + 4, :, :],
                in_=keys_scales[0, 8 * pair : 8 * pair + 8, :].bitcast(I32).rearrange("(a r) n -> r a n", a=2),
            )
        factor = sb.tile([P, PACK], F32, name="factor")
        nc.scalar.dma_start(out=factor[:], in_=slot_factor.rearrange("o (p t) -> p (o t)", t=PACK))
        wm_raw = load_rows("wm_raw", wm)
        ms_raw = [load_rows("ms_raw%d" % h, mstore[:, h * BANK : (h + 1) * BANK]) for h in range(m_halves)]
        key_words = sb.tile([P, T], U32, name="key_words", align_bytes=64)
        nc.sync.dma_start(
            out=key_words[:].bitcast(I32), in_=keys_words[0].rearrange("p n t -> p (n t)").bitcast(I32)
        )
        list3 = load_list("list3", offs3)
        q_raw = load_rows("q_raw", query)
        list2 = load_list("list2", offs2)
        earl_sb = [load_block("earl%d" % qb, earl[qb * P : (qb + 1) * P, :]) for qb in range(q_blocks)]
        vals_sb = [load_block("vals%d" % eb, vals[eb * P : (eb + 1) * P, :]) for eb in range(e_blocks)]

        for quad in range(4):
            first = 64 * (quad // 2)
            nc.vector.tensor_copy(
                key_bytes[32 * quad : 32 * quad + 4, :].bitcast(I32), byte_rows[first : first + 4, quad % 2, :]
            )
        picked_bytes = sb.tile([P, I], U8, name="picked_bytes", align_bytes=64)
        nc.vector.tensor_copy(picked_bytes[:], key_bytes[:].indirect(list1[:]))

        wm_q = quantize("wm", interleave("wm_bf", wm_raw, 256))
        me_sb = [sb.tile([P, M], F32, name="me%d" % eb) for eb in range(e_blocks)]
        def memories(h, ms_q):
            for eb in range(e_blocks):
                me_ps = psum.tile([P, BANK], F32, name="me_ps", tag="block%d" % eb)
                product(me_ps[:], wm_q, slice(eb * P, (eb + 1) * P), ms_q)
                if h == 1 and eb >= 2:
                    nc.vector.tensor_copy(out=me_sb[eb][:, h * BANK : (h + 1) * BANK], in_=me_ps[:])
                else:
                    nc.scalar.copy(out=me_sb[eb][:, h * BANK : (h + 1) * BANK], in_=me_ps[:])

        memories(0, quantize("ms0", interleave("ms_bf0", ms_raw[0], 176)))
        ms1_q = quantize("ms1", interleave("ms_bf1", ms_raw[1]))

        picked_words = sb.tile([P, I], U32, name="picked_words", align_bytes=64)
        nc.vector.tensor_copy(picked_words[:], key_words[:].indirect(list1[:]))
        q_q = quantize("q", interleave("q_bf", q_raw))
        scores = []
        for qb in range(q_blocks):
            a_ps = psum.tile([P, I], F32, name="a_ps", tag="score%d" % qb)
            product(a_ps[:], q_q, slice(qb * P, (qb + 1) * P), (picked_words, picked_bytes))
            scores.append(a_ps)

        w_bf = sb.tile([P, Q, PACK], BF16, name="w_bf", align_bytes=64)
        w_rows = []
        for qb in range(q_blocks):
            earl_picked = sb.tile([P, I], F32, name="earl_picked%d" % qb)
            nc.scalar.activation(earl_picked[:], earl_sb[qb][:].indirect(list2[:]), COPY)
            w_row = sb.tile([P, I], F32, name="w_row%d" % qb)
            nc.vector.tensor_tensor(
                w_row[:].rearrange("p (t c i) -> p c t i", t=PACK, i=4),
                scores[qb][:].rearrange("p (c i t) -> p c t i", t=PACK, i=4),
                earl_picked[:].rearrange("p (c i t) -> p c t i", t=PACK, i=4),
                MULT,
            )
            w_rows.append(w_row)
        for qb in range(q_blocks):
            wt_ps = psum.tile([P, PACK, P], F32, name="wt_ps", tag="score%d" % qb)
            for t in range(PACK):
                nc.tensor.transpose(wt_ps[:, t, :], w_rows[qb][:, t * P : (t + 1) * P], ident[:])
            nc.vector.tensor_tensor(
                w_bf[:, qb * P : (qb + 1) * P, :],
                wt_ps[:].rearrange("p t q -> p q t"),
                factor[:].unsqueeze(1).to_broadcast([P, P, PACK]),
                MULT,
            )
        w_q = quantize("w", w_bf)

        memories(1, ms1_q)
        picked_by_scalar = sb.tile([P, 2, Q], F32, name="picked_by_scalar", tag="earl1", align_bytes=64)
        picked_by_vector = sb.tile([P, 2, Q], F32, name="picked_by_vector", tag="w_bf", align_bytes=64)
        me_picked = []
        for eb in range(e_blocks):
            if eb < 2:
                picked = picked_by_scalar[:, eb, :]
                nc.scalar.activation(picked, me_sb[eb][:].indirect(list3[:]), COPY)
            else:
                picked = picked_by_vector[:, eb - 2, :]
                nc.vector.tensor_copy(picked, me_sb[eb][:].indirect(list3[:]))
            me_picked.append(picked)

        def turn_values(eb):
            v_picked = sb.tile([P, I], BF16, name="v_picked%d" % eb)
            if eb < e_blocks - 2:
                nc.scalar.activation(v_picked[:], vals_sb[eb][:].indirect(list1[:]), COPY)
            else:
                half = I // 2
                nc.scalar.activation(v_picked[:, :half], vals_sb[eb][:].indirect(list1[:, : half // 16]), COPY)
                nc.vector.tensor_copy(v_picked[:, half:], vals_sb[eb][:].indirect(list1[:, half // 16 :]))
            pairs = v_picked[:].bitcast(F32)
            vt_ps = psum.tile([P, 2, P], F32, name="vt_ps", tag="block%d" % eb)
            for u in range(2):
                nc.tensor.transpose(vt_ps[:, u, :], pairs[:, u : I // 2 : 2], ident[:])
            v_bf = sb.tile([P, P, PACK], BF16, name="v_bf", tag="vals%d" % ((eb + 1) % e_blocks), align_bytes=64)
            nc.scalar.copy(out=v_bf[:].bitcast(F32), in_=vt_ps[:].rearrange("p u e -> p e u"))
            return quantize("v%d" % eb, v_bf)

        def finish(eb, v_q):
            o_ps = psum.tile([P, Q], F32, name="o_ps", tag="score%d" % (eb % 2))
            product(o_ps[:], v_q, slice(0, P), w_q)
            result = sb.tile([P, Q], F32, name="result", tag="vals%d" % ((eb + 2) % e_blocks), align_bytes=64)
            nc.vector.tensor_tensor(result[:], o_ps[:], me_picked[eb], MULT)
            nc.sync.dma_start(out=out[eb * P : (eb + 1) * P, :], in_=result[:])

        v_q = [turn_values(0)]
        for eb in range(1, e_blocks):
            v_q.append(turn_values(eb))
        for eb in range(e_blocks):
            finish(eb, v_q[eb])
